import numpy as np
import ml_dtypes


def mxq(x, axis, fmt="e4m3"):
    dtype, down = {"e4m3": (ml_dtypes.float8_e4m3fn, 7), "e5m2": (ml_dtypes.float8_e5m2, 14)}[fmt]
    v = np.moveaxis(np.asarray(x, np.float32).astype(ml_dtypes.bfloat16).astype(np.float64), axis, -1)
    blocks = v.reshape(v.shape[:-1] + (-1, 32))
    amax = np.abs(blocks).max(-1, keepdims=True)
    byte = np.maximum(np.where(amax > 0, np.frexp(amax)[1] - 1 + 127, 0) - down, 1)
    scale = np.exp2(byte - 127.0)
    codes = (blocks / scale).astype(np.float32).astype(dtype).astype(np.float64)
    return np.moveaxis((codes * scale).reshape(v.shape), -1, axis)


WIDE = False


def mx_kscale(k):
    if not WIDE:
        return np.ones(k)
    levels = np.array([10, -10, 5, -5, 0])
    if k % 512:
        return np.exp2(np.random.permutation(np.resize(levels, k // 32))).repeat(32)
    a = np.empty((k // 512, 16))
    for p in range(k // 512):
        a[p, :8] = np.random.permutation(np.resize(levels, 8))
        for g in range(8):
            far = levels[np.abs(levels - a[p, g]) >= 10]
            a[p, g + 8] = far[np.random.randint(len(far))]
    return np.exp2(a.ravel()).repeat(32)


def f64(x):
    return np.asarray(x).astype(np.float64)


def striped(idx):
    return np.tile(idx.reshape(-1, 16).T, (8, 1)).astype(np.uint16)


def unstriped(offs):
    return offs[:16].T.reshape(-1).astype(np.int64)


E2M1 = np.array([0.0, 0.5, 1.0, 1.5, 2.0, 3.0, 4.0, 6.0, -0.0, -0.5, -1.0, -1.5, -2.0, -3.0, -4.0, -6.0])


def pack_weight(w, fmt):
    k, n = w.shape
    w = f64(np.asarray(w, np.float32).astype(ml_dtypes.bfloat16)).reshape(k // 32, 32, n)
    amax = np.abs(w).max(1)
    if fmt == "e4m3":
        byte = np.frexp(amax)[1] - 1 + 127 - 7
    else:
        mant, ex = np.frexp(amax / 6.0)
        byte = np.where(mant > 0.5, ex, ex - 1) + 127
    byte = np.clip(np.where(amax > 0, byte, 1), 1, 254)
    scaled = (w * np.exp2(127.0 - byte)[:, None, :]).reshape(k, n).astype(np.float32)
    by_word = np.ascontiguousarray(scaled.reshape(k // 512, 128, 4, n).transpose(0, 1, 3, 2))
    if fmt == "e4m3":
        words = by_word.astype(ml_dtypes.float8_e4m3fn).view(np.uint8)
    else:
        c = by_word.astype(ml_dtypes.float4_e2m1fn).view(np.uint8) & 0xF
        words = (c[..., 0::2] | (c[..., 1::2] << 4)).reshape(k // 512, 128, 2 * n)
    return np.ascontiguousarray(words), np.ascontiguousarray(byte.astype(np.uint8).reshape(k // 512, 16, n))


def unpack_weight(words, scales, fmt):
    g, _, n = scales.shape
    words = np.ascontiguousarray(words).reshape(g, 128, n, -1)
    if fmt == "e4m3":
        vals = words.view(ml_dtypes.float8_e4m3fn).astype(np.float64)
    else:
        nib = np.empty((g, 128, n, 4), np.uint8)
        nib[..., 0::2] = words & 0xF
        nib[..., 1::2] = words >> 4
        vals = E2M1[nib]
    vals = vals * np.repeat(np.exp2(scales.astype(np.float64) - 127.0), 8, axis=1)[..., None]
    return vals.transpose(0, 1, 3, 2).reshape(g * 512, n)


def gelu(v):
    return 0.5 * v * (1.0 + np.tanh(np.sqrt(2.0 / np.pi) * (v + 0.044715 * v**3)))


K, H, T, S, T2, P = 1024, 1024, 2048, 512, 1024, 512


def setup_inputs():
    n = np.random.standard_normal
    s = mx_kscale(K)[:, None]
    u = mx_kscale(H)[:, None]
    d = {}
    d["tab_words"], d["tab_scales"] = pack_weight(n((K, T)) * s, "e4m3")
    d["offs"] = striped(np.random.permutation(T)[:S])
    d["w1"] = (n((K, H)) / s * u.T / K ** 0.5).astype(np.float32)
    d["w2_words"], d["w2_scales"] = pack_weight(n((K, H)) / s * u.T / K ** 0.5, "e2m1")
    d["w3_words"], d["w3_scales"] = pack_weight(0.8 * n((K, H)) / s * u.T / K ** 0.5, "e4m3")
    d["wgs"] = np.exp(0.3 * n((128, S))).astype(np.float32)
    d["page0"] = (n((H, T2)) * u).astype(np.float32)
    d["offs2"] = striped(np.random.permutation(T2)[:S])
    d["offs3"] = striped(np.random.permutation(T2)[:P])
    d["gain"] = np.random.uniform(-1.0, 0.5, H).astype(np.float32)
    d["sense"] = (0.6 * n(H) / H ** 0.5 / u[:, 0] ** 2).astype(np.float32)
    d["base"] = n((T2, P)).astype(np.float32)
    return d


def reference(tab_words, tab_scales, offs, w1, w2_words, w2_scales, w3_words, w3_scales,
              wgs, page0, offs2, offs3, gain, sense, base):
    v = unpack_weight(tab_words, tab_scales, "e4m3")[:, unstriped(offs)]
    a = mxq(f64(w1), 0, "e4m3").T @ v
    b = unpack_weight(w2_words, w2_scales, "e2m1").T @ v
    c = unpack_weight(w3_words, w3_scales, "e4m3").T @ v
    h = np.maximum(a, b) - c
    page = f64(page0).copy()
    page[:, unstriped(offs2)] = np.tile(f64(wgs), (H // 128, 1)) * h
    x0 = page[:, unstriped(offs3)]
    x = np.maximum(x0, f64(gain)[:, None] * x0) * f64(sense)[:, None]
    e = mxq(page, 0, "e4m3").T @ mxq(x, 0, "e4m3")
    return (e - f64(base)) ** 2

@@ -1,0 +1,324 @@
+from contextlib import ExitStack
+
+import concourse.mybir as mybir
+from concourse.masks import make_identity
+
+K, H, T, S, T2, NP = 1024, 1024, 2048, 512, 1024, 512
+FLOPS = 2 * 3 * K * H * S + 2 * H * T2 * NP
+
+F32 = mybir.dt.float32
+BF16 = mybir.dt.bfloat16
+I32 = mybir.dt.int32
+U32 = mybir.dt.uint32
+U16 = mybir.dt.uint16
+U8 = mybir.dt.uint8
+FP8X4 = mybir.dt.float8_e4m3fn_x4
+FP4X4 = mybir.dt.float4_e2m1fn_x4
+ALU = mybir.AluOpType
+ACT = mybir.ActivationFunctionType
+
+P = 128
+W2_PLANE, W3_PLANE, PLANES = 0, 2048, 4096
+
+
+def tile_list_sign_variant_check_kernel(tc, tab_words, tab_scales, offs, w1, w2_words, w2_scales,
+                                                  w3_words, w3_scales, wgs, page0, offs2, offs3, gain, sense,
+                                                  base, out):
+    nc = tc.nc
+    with ExitStack() as ctx:
+        keep = ctx.enter_context(tc.tile_pool(name="keep", bufs=1))
+        work = ctx.enter_context(tc.tile_pool(name="work", bufs=2))
+        psum = ctx.enter_context(tc.psum_pool(name="psum", bufs=8))
+
+        def bank():
+            return psum.tile([P, 512], F32, name="bank")
+
+        list1 = keep.tile([P, S // 16], U16, name="list1")
+        list2 = keep.tile([P, S // 16], U16, name="list2")
+        list3 = keep.tile([P, NP // 16], U16, name="list3")
+        tab_bytes = keep.tile([P, 2, T], U8, name="tab_bytes", align_bytes=64)
+        w_bytes = keep.tile([P, 4096], U8, name="w_bytes", align_bytes=64)
+        planes = keep.tile([P, PLANES], U8, name="planes", align_bytes=64)
+        wgs_raw = keep.tile([P, S], F32, name="wgs_raw")
+        row_vecs = keep.tile([P, 256], F32, name="row_vecs")
+        ident = keep.tile([P, P], F32, name="ident")
+        tab = [keep.tile([P, T], U32, name="tab%d" % a, align_bytes=64) for a in range(2)]
+        pages = [keep.tile([P, T2], F32, name="page%d" % i) for i in range(8)]
+        page_rows = page0.rearrange("(b g t j) m -> b t g j m", b=2, g=16, t=4, j=8)
+
+        def load_w1(b, a):
+            raw = work.tile([P, 4, 512], F32, name="big", bufs=3)
+            nc.sync.dma_start(out=raw[:], in_=w1[512 * a:512 * (a + 1), 512 * b:512 * (b + 1)].rearrange("(p i) c -> p i c", i=4))
+            return raw
+
+        def load_w23(b):
+            raw3 = work.tile([P, 2, 512], U32, name="w3_raw")
+            nc.sync.dma_start(out=raw3[:].bitcast(I32),
+                              in_=w3_words[:, :, 512 * b:512 * (b + 1), :].rearrange("a p c i -> p a (c i)").bitcast(I32))
+            raw2 = work.tile([P, 2, 256], U32, name="w2_raw")
+            nc.sync.dma_start(out=raw2[:].bitcast(I32),
+                              in_=w2_words[:, :, 1024 * b:1024 * (b + 1)].rearrange("a p c -> p a c").bitcast(I32))
+            return raw2, raw3
+
+        def load_tab(a):
+            nc.sync.dma_start(out=tab[a][:].bitcast(I32), in_=tab_words[a].rearrange("p t i -> p (t i)").bitcast(I32))
+
+        def load_page(i):
+            nc.sync.dma_start(out=pages[i][:], in_=page_rows[i // 4, i % 4])
+
+        def load_w_scales(w, scales):
+            for q in range(4):
+                nc.sync.dma_start(out=w_bytes[32 * q:32 * q + 4, 2048 * w:2048 * (w + 1)].rearrange("r (a c) -> r a c", a=2).bitcast(I32),
+                                  in_=scales[:, 4 * q:4 * q + 4, :].rearrange("a r c -> r a c").bitcast(I32))
+
+        load_tab(0)
+        nc.sync.dma_start(out=wgs_raw[:], in_=wgs)
+        nc.sync.dma_start(out=list1[:], in_=offs)
+        w1_raw = {(0, 0): load_w1(0, 0)}
+        load_w_scales(0, w2_scales)
+        w23_raw = [load_w23(0)]
+        load_w_scales(1, w3_scales)
+        load_tab(1)
+        w1_raw[0, 1] = load_w1(0, 1)
+        load_page(0)
+        nc.sync.dma_start(out=list2[:], in_=offs2)
+        nc.sync.dma_start(out=list3[:], in_=offs3)
+        nc.vector.memset(tab_bytes[:].bitcast(I32), 0)
+        nc.vector.memset(planes[:].bitcast(I32), 0)
+        nc.vector.memset(row_vecs[:], 0.0)
+        for v, vec in enumerate((gain, sense)):
+            nc.sync.dma_start(out=row_vecs[4 * v:4 * v + 4, :].rearrange("t (x j) -> t x j", j=8),
+                              in_=vec.rearrange("(x t j) -> t x j", t=4, j=8))
+        load_page(1)
+        w1_raw[1, 0] = load_w1(1, 0)
+        load_page(2)
+        w1_raw[1, 1] = load_w1(1, 1)
+        load_page(3)
+        w23_raw.append(load_w23(1))
+        for i in range(4, 8):
+            load_page(i)
+        base_sb = []
+        for half in range(2):
+            rows = work.tile([P, 4, 512], F32, name="big", bufs=3)
+            nc.sync.dma_start(out=rows[:], in_=base[512 * half:512 * (half + 1), :].rearrange("(k p) n -> p k n", p=P))
+            base_sb.append(rows)
+
+        make_identity(nc, ident[:])
+        for q in range(4):
+            nc.gpsimd.dma_start(out=tab_bytes[32 * q:32 * q + 4].bitcast(I32),
+                                in_=tab_scales[:, 4 * q:4 * q + 4, :].rearrange("a r t -> r a t").bitcast(I32))
+        picked_bytes = keep.tile([P, 2, S], U8, name="picked_bytes", align_bytes=64)
+
+        def gather_bytes(a):
+            nc.vector.tensor_copy(out=picked_bytes[:, a, :], in_=tab_bytes[:, a, :].indirect(list1[:]))
+
+        def deal_w_scales(b, engine_copy, word):
+            for q in range(4):
+                rows = slice(32 * q, 32 * q + 4)
+                dst = planes[rows].bitcast(word).rearrange("r (x b t g w) -> r b x t g w", b=2, t=4, g=16, w=2)
+                src = w_bytes[rows].bitcast(word).rearrange("r (x b g t w) -> r b x t g w", b=2, t=4, g=16, w=2)
+                engine_copy(out=dst[:, b], in_=src[:, b])
+
+        turned = bank()
+        for c in range(4):
+            nc.tensor.transpose(turned[:, P * c:P * (c + 1)], wgs_raw[:, P * c:P * (c + 1)], ident[:])
+        wgs_cols = keep.tile([P, 4, 4, P], F32, name="wgs_cols")
+        for c in range(4):
+            src = turned[:, P * c:P * (c + 1)].rearrange("j (g t i) -> j t g i", g=4, t=4).unsqueeze(2).to_broadcast([P, 4, 4, 4, 8])
+            nc.scalar.copy(out=wgs_cols[:, c].rearrange("j t (q g i) -> j t q g i", q=4, g=4), in_=src)
+        wgs_rows = keep.tile([P, 4, S], F32, name="wgs_rows")
+        for t in range(4):
+            back = bank()
+            for c in range(4):
+                nc.tensor.transpose(back[:, P * c:P * (c + 1)], wgs_cols[:, c, t, :], ident[:])
+            nc.scalar.copy(out=wgs_rows[:, t, :], in_=back[:])
+
+        picked = []
+        for a in range(2):
+            words = keep.tile([P, S], U32, name="picked%d" % a, align_bytes=64)
+            picked.append(words)
+
+        def gather_words(a):
+            nc.vector.tensor_copy(out=picked[a][:], in_=tab[a][:].indirect(list1[:]))
+
+        w1_codes = {}
+        w1_scales = {}
+
+        def prepare_w1(b, a, engines, quant_slots):
+            raw = w1_raw[b, a][:].rearrange("p i (g t j) -> p t g j i", g=16, t=4)
+            grouped = work.tile([P, 4, 512], BF16, name="w1_bf16", align_bytes=64)
+            codes = keep.tile([P, 512], U32, name="w1_codes%d%d" % (b, a), align_bytes=64)
+            scales = keep.tile([P, 512], U8, name="w1_scales%d%d" % (b, a), align_bytes=64)
+            w1_codes[b, a], w1_scales[b, a] = codes, scales
+            for t in range(4):
+                dst = grouped[:, t, :].rearrange("p (g j i) -> p g j i", g=16, j=8)
+                if engines[t] == "v":
+                    nc.vector.tensor_copy(out=dst, in_=raw[:, t])
+                else:
+                    nc.scalar.copy(out=dst, in_=raw[:, t])
+                if (t + 1) % quant_slots == 0:
+                    t0 = t + 1 - quant_slots
+                    nc.vector.quantize_mx(out=codes[:, P * t0:P * (t + 1)].bitcast(FP8X4), scales=scales[:, P * t0:P * (t + 1)],
+                                          in_=grouped[:, t0:t + 1, :].rearrange("p t c -> p (t c)"))
+
+        w2_codes, w3_codes = [], []
+
+        def prepare_w23(b):
+            raw2, raw3 = w23_raw[b]
+            codes2 = keep.tile([P, 2, 1024], U8, name="w2_codes%d" % b, align_bytes=64)
+            nc.scalar.copy(out=codes2[:].bitcast(U32).rearrange("p a (t g w) -> p a t g w", t=4, g=16),
+                           in_=raw2[:].rearrange("p a (g t w) -> p a t g w", t=4, g=16))
+            codes3 = keep.tile([P, 2, 512], U32, name="w3_codes%d" % b, align_bytes=64)
+            nc.scalar.copy(out=codes3[:].rearrange("p a (t g w) -> p a t g w", t=4, g=16),
+                           in_=raw3[:].rearrange("p a (g t w) -> p a t g w", t=4, g=16))
+            w2_codes.append(codes2)
+            w3_codes.append(codes3)
+
+        gather_words(0)
+        gather_bytes(0)
+        gather_bytes(1)
+        prepare_w1(0, 0, "vvvv", 4)
+        deal_w_scales(0, nc.vector.tensor_copy, I32)
+        prepare_w23(0)
+        gather_words(1)
+        prepare_w1(0, 1, "vvss", 1)
+
+        vec_bank = bank()
+        for b in range(2):
+            nc.tensor.transpose(vec_bank[:, P * b:P * (b + 1)], row_vecs[:, P * b:P * (b + 1)], ident[:])
+        row_consts = keep.tile([P, 2, 8], F32, name="row_consts")
+        nc.scalar.copy(out=row_consts[:], in_=vec_bank[:, 0:2 * P].rearrange("p (b c) -> p b c", b=2)[:, :, 0:8])
+
+        def product(lhs_codes, lhs_scales):
+            acc = bank()
+            for a in range(2):
+                nc.tensor.matmul_mx(out=acc[:], lhsT=lhs_codes(a), lhsT_scale=lhs_scales(a), rhs=picked[a][:].bitcast(FP8X4),
+                                    rhs_scale=picked_bytes[:, a, :], start=(a == 0), stop=(a == 1))
+            return acc
+
+        sums = {}
+        larger = {}
+        feats = {}
+
+        def first_products(i):
+            b, t = divmod(i, 4)
+            col = 512 * b + P * t
+            second = product(lambda a: w2_codes[b][:, a, 256 * t:256 * (t + 1)].bitcast(FP4X4),
+                             lambda a: planes[:, W2_PLANE + 1024 * a + col:W2_PLANE + 1024 * a + col + P])
+            third = product(lambda a: w3_codes[b][:, a, P * t:P * (t + 1)].bitcast(FP8X4),
+                            lambda a: planes[:, W3_PLANE + 1024 * a + col:W3_PLANE + 1024 * a + col + P])
+            first = product(lambda a: w1_codes[b, a][:, P * t:P * (t + 1)].bitcast(FP8X4),
+                            lambda a: w1_scales[b, a][:, P * t:P * (t + 1)])
+            second_sb = work.tile([P, S], F32, name="second_sb")
+            nc.scalar.copy(out=second_sb[:], in_=second[:])
+            sums[i] = (first, second_sb, third)
+
+        def take_max(i):
+            first, second_sb, third = sums[i]
+            larger[i] = work.tile([P, S], F32, name="larger")
+            nc.vector.tensor_tensor(out=larger[i][:], in0=first[:], in1=second_sb[:], op=ALU.max)
+
+        def take_off(i):
+            feats[i] = work.tile([P, S], F32, name="feat", bufs=3)
+            nc.vector.tensor_tensor(out=feats[i][:], in0=larger[i][:], in1=sums[i][2][:], op=ALU.subtract)
+
+        def scatter(i):
+            nc.vector.tensor_tensor(out=pages[i][:].indirect(list2[:]), in0=feats[i][:], in1=wgs_rows[:, i % 4, :], op=ALU.mult)
+
+        page_pairs = [work.tile([P, 2, T2, 2], BF16, name="page_pairs", bufs=1, align_bytes=64) for b in range(2)]
+        x_pairs = [work.tile([P, 2, NP, 2], BF16, name="x_pairs", bufs=1, align_bytes=64) for b in range(2)]
+        page_codes = [keep.tile([P, T2], U32, name="page_codes%d" % b, align_bytes=64) for b in range(2)]
+        page_scales = [keep.tile([P, T2], U8, name="page_scales%d" % b, align_bytes=64) for b in range(2)]
+        x_codes = [keep.tile([P, NP], U32, name="x_codes%d" % b, align_bytes=64) for b in range(2)]
+        x_scales = [keep.tile([P, NP], U8, name="x_scales%d" % b, align_bytes=64) for b in range(2)]
+        heads = {}
+        bent = {}
+
+        def round_page(i):
+            b, t = divmod(i, 4)
+            nc.scalar.copy(out=page_pairs[b][:, t // 2, :, t % 2], in_=pages[i][:])
+
+        def fetch(i):
+            heads[i] = work.tile([P, NP], F32, name="head")
+            nc.vector.tensor_copy(out=heads[i][:], in_=pages[i][:].indirect(list3[:]))
+
+        def bend(i):
+            b, t = divmod(i, 4)
+            bent[i] = work.tile([P, NP], F32, name="bent")
+            nc.vector.scalar_tensor_tensor(out=bent[i][:], in0=heads[i][:], scalar=row_consts[:, b, t:t + 1], in1=heads[i][:],
+                                           op0=ALU.mult, op1=ALU.max)
+
+        def round_x(i):
+            b, t = divmod(i, 4)
+            dst = x_pairs[b][:, t // 2, :, t % 2]
+            factor = row_consts[:, b, 4 + t:5 + t]
+            if i >= 6:
+                nc.vector.tensor_scalar(out=dst, in0=bent[i][:], scalar1=factor, scalar2=None, op0=ALU.mult)
+            else:
+                nc.scalar.activation(out=dst, in_=bent[i][:], func=ACT.Copy, scale=factor)
+
+        def weave(pairs, cols, engine_copy, word=U32):
+            width = cols.stop - cols.start
+            woven = work.tile([P, 4 * width], BF16, name="woven", bufs=4, align_bytes=64)
+            words = pairs[:].rearrange("p u c e -> p u (c e)").bitcast(word)[:, :, cols]
+            engine_copy(out=woven[:].bitcast(word).rearrange("p (c u) -> p c u", u=2), in_=words.rearrange("p u c -> p c u"))
+            return woven
+
+        def quantise(woven, codes, scales, cols):
+            nc.vector.quantize_mx(out=codes[:, cols].bitcast(FP8X4), scales=scales[:, cols], in_=woven[:])
+
+        first_products(0)
+        take_max(0)
+        take_off(0)
+        first_products(1)
+        take_max(1)
+        take_off(1)
+        woven_pages, woven_x = {}, {}
+        for i in range(8):
+            if i == 1:
+                prepare_w23(1)
+                deal_w_scales(1, nc.scalar.copy, U32)
+                prepare_w1(1, 0, "ssss", 4)
+            if i == 2:
+                prepare_w1(1, 1, "ssss", 4)
+            scatter(i)
+            round_page(i)
+            if i + 2 < 8:
+                first_products(i + 2)
+                take_max(i + 2)
+            fetch(i)
+            if i + 2 < 8:
+                take_off(i + 2)
+            bend(i)
+            round_x(i)
+            if i == 3:
+                for c in range(2):
+                    woven_pages[c] = weave(page_pairs[0], slice(512 * c, 512 * (c + 1)), nc.scalar.copy)
+                woven_x[0] = weave(x_pairs[0], slice(0, NP), nc.scalar.copy)
+            if i == 4:
+                for c in range(2):
+                    quantise(woven_pages[c], page_codes[0], page_scales[0], slice(512 * c, 512 * (c + 1)))
+                quantise(woven_x[0], x_codes[0], x_scales[0], slice(0, NP))
+
+        def score(acc, b, k):
+            nc.tensor.matmul_mx(out=acc[:], lhsT=page_codes[b][:, P * k:P * (k + 1)].bitcast(FP8X4),
+                                lhsT_scale=page_scales[b][:, P * k:P * (k + 1)], rhs=x_codes[b][:].bitcast(FP8X4),
+                                rhs_scale=x_scales[b][:], start=(b == 0), stop=(b == 1))
+
+        scores = [bank() for k in range(8)]
+        for k in range(8):
+            score(scores[k], 0, k)
+        woven_x[1] = weave(x_pairs[1], slice(0, NP), nc.vector.tensor_copy, I32)
+        for c in range(4):
+            woven_pages[c] = weave(page_pairs[1], slice(256 * c, 256 * (c + 1)), nc.scalar.copy)
+        quantise(woven_pages[0], page_codes[1], page_scales[1], slice(0, 256))
+        quantise(woven_x[1], x_codes[1], x_scales[1], slice(0, NP))
+        for c in range(1, 4):
+            quantise(woven_pages[c], page_codes[1], page_scales[1], slice(256 * c, 256 * (c + 1)))
+        for k in range(8):
+            score(scores[k], 1, k)
+            diff = work.tile([P, NP], F32, name="diff", bufs=3)
+            nc.vector.tensor_tensor(out=diff[:], in0=scores[k][:], in1=base_sb[k // 4][:, k % 4, :], op=ALU.subtract)
+            result = work.tile([P, NP], F32, name="result", bufs=4)
+            nc.scalar.activation(out=result[:], in_=diff[:], func=ACT.Square)
+            nc.sync.dma_start(out=out[P * k:P * (k + 1), :], in_=result[:])

@@ -18,7 +18,7 @@ ALU = mybir.AluOpType
 ACT = mybir.ActivationFunctionType
 
 P = 128
-W2_PLANE, W3_PLANE, PLANES = 0, 2048, 4096
+PLANES = 2048
 
 
 def tile_list_sign_variant_check_kernel(tc, tab_words, tab_scales, offs, w1, w2_words, w2_scales,
@@ -37,7 +37,7 @@ def tile_list_sign_variant_check_kernel(tc, tab_words, tab_scales, offs, w1, w2_
         list2 = keep.tile([P, S // 16], U16, name="list2")
         list3 = keep.tile([P, NP // 16], U16, name="list3")
         tab_bytes = keep.tile([P, 2, T], U8, name="tab_bytes", align_bytes=64)
-        w_bytes = keep.tile([P, 4096], U8, name="w_bytes", align_bytes=64)
+        w_bytes = keep.tile([P, PLANES], U8, name="w_bytes", align_bytes=64)
         planes = keep.tile([P, PLANES], U8, name="planes", align_bytes=64)
         wgs_raw = keep.tile([P, S], F32, name="wgs_raw")
         row_vecs = keep.tile([P, 256], F32, name="row_vecs")
@@ -66,18 +66,20 @@ def tile_list_sign_variant_check_kernel(tc, tab_words, tab_scales, offs, w1, w2_
         def load_page(i):
             nc.sync.dma_start(out=pages[i][:], in_=page_rows[i // 4, i % 4])
 
-        def load_w_scales(w, scales):
-            for q in range(4):
-                nc.sync.dma_start(out=w_bytes[32 * q:32 * q + 4, 2048 * w:2048 * (w + 1)].rearrange("r (a c) -> r a c", a=2).bitcast(I32),
-                                  in_=scales[:, 4 * q:4 * q + 4, :].rearrange("a r c -> r a c").bitcast(I32))
+        def load_w_scales(quadrants):
+            for w, scales in enumerate((w2_scales, w3_scales)):
+                for q in quadrants:
+                    nc.sync.dma_start(out=w_bytes[32 * q + 4 * w:32 * q + 4 * w + 4, :].rearrange("r (a c) -> r a c", a=2).bitcast(I32),
+                                      in_=scales[:, 4 * q:4 * q + 4, :].rearrange("a r c -> r a c").bitcast(I32))
 
+        nc.gpsimd.memset(row_vecs[:], 0.0)
         load_tab(0)
         nc.sync.dma_start(out=wgs_raw[:], in_=wgs)
         nc.sync.dma_start(out=list1[:], in_=offs)
         w1_raw = {(0, 0): load_w1(0, 0)}
-        load_w_scales(0, w2_scales)
+        load_w_scales((0, 2))
         w23_raw = [load_w23(0)]
-        load_w_scales(1, w3_scales)
+        load_w_scales((1, 3))
         load_tab(1)
         w1_raw[0, 1] = load_w1(0, 1)
         load_page(0)
@@ -85,26 +87,27 @@ def tile_list_sign_variant_check_kernel(tc, tab_words, tab_scales, offs, w1, w2_
         nc.sync.dma_start(out=list3[:], in_=offs3)
         nc.vector.memset(tab_bytes[:].bitcast(I32), 0)
         nc.vector.memset(planes[:].bitcast(I32), 0)
-        nc.vector.memset(row_vecs[:], 0.0)
         for v, vec in enumerate((gain, sense)):
             nc.sync.dma_start(out=row_vecs[4 * v:4 * v + 4, :].rearrange("t (x j) -> t x j", j=8),
                               in_=vec.rearrange("(x t j) -> t x j", t=4, j=8))
-        load_page(1)
-        w1_raw[1, 0] = load_w1(1, 0)
-        load_page(2)
-        w1_raw[1, 1] = load_w1(1, 1)
-        load_page(3)
-        w23_raw.append(load_w23(1))
-        for i in range(4, 8):
-            load_page(i)
         base_sb = []
-        for half in range(2):
+
+        def load_base(half):
             rows = work.tile([P, 4, 512], F32, name="big", bufs=3)
             nc.sync.dma_start(out=rows[:], in_=base[512 * half:512 * (half + 1), :].rearrange("(k p) n -> p k n", p=P))
             base_sb.append(rows)
 
+        w1_raw[1, 0] = load_w1(1, 0)
+        load_page(1)
+        w1_raw[1, 1] = load_w1(1, 1)
+        w23_raw.append(load_w23(1))
+        load_base(0)
+        for i in range(2, 8):
+            load_page(i)
+        load_base(1)
+
         make_identity(nc, ident[:])
-        for q in range(4):
+        for q in (0, 2, 1, 3):
             nc.gpsimd.dma_start(out=tab_bytes[32 * q:32 * q + 4].bitcast(I32),
                                 in_=tab_scales[:, 4 * q:4 * q + 4, :].rearrange("a r t -> r a t").bitcast(I32))
         picked_bytes = keep.tile([P, 2, S], U8, name="picked_bytes", align_bytes=64)
@@ -114,7 +117,7 @@ def tile_list_sign_variant_check_kernel(tc, tab_words, tab_scales, offs, w1, w2_
 
         def deal_w_scales(b, engine_copy, word):
             for q in range(4):
-                rows = slice(32 * q, 32 * q + 4)
+                rows = slice(32 * q, 32 * q + 8)
                 dst = planes[rows].bitcast(word).rearrange("r (x b t g w) -> r b x t g w", b=2, t=4, g=16, w=2)
                 src = w_bytes[rows].bitcast(word).rearrange("r (x b g t w) -> r b x t g w", b=2, t=4, g=16, w=2)
                 engine_copy(out=dst[:, b], in_=src[:, b])
@@ -144,22 +147,21 @@ def tile_list_sign_variant_check_kernel(tc, tab_words, tab_scales, offs, w1, w2_
         w1_codes = {}
         w1_scales = {}
 
-        def prepare_w1(b, a, engines, quant_slots):
+        def w1_tiles(b, a):
             raw = w1_raw[b, a][:].rearrange("p i (g t j) -> p t g j i", g=16, t=4)
             grouped = work.tile([P, 4, 512], BF16, name="w1_bf16", align_bytes=64)
             codes = keep.tile([P, 512], U32, name="w1_codes%d%d" % (b, a), align_bytes=64)
             scales = keep.tile([P, 512], U8, name="w1_scales%d%d" % (b, a), align_bytes=64)
             w1_codes[b, a], w1_scales[b, a] = codes, scales
-            for t in range(4):
-                dst = grouped[:, t, :].rearrange("p (g j i) -> p g j i", g=16, j=8)
-                if engines[t] == "v":
-                    nc.vector.tensor_copy(out=dst, in_=raw[:, t])
-                else:
-                    nc.scalar.copy(out=dst, in_=raw[:, t])
-                if (t + 1) % quant_slots == 0:
-                    t0 = t + 1 - quant_slots
-                    nc.vector.quantize_mx(out=codes[:, P * t0:P * (t + 1)].bitcast(FP8X4), scales=scales[:, P * t0:P * (t + 1)],
-                                          in_=grouped[:, t0:t + 1, :].rearrange("p t c -> p (t c)"))
+            return raw, grouped
+
+        def round_w1(parts, t, engine_copy):
+            raw, grouped = parts
+            engine_copy(out=grouped[:, t, :].rearrange("p (g j i) -> p g j i", g=16, j=8), in_=raw[:, t])
+
+        def quantise_w1(b, a, parts, t0, t1):
+            nc.vector.quantize_mx(out=w1_codes[b, a][:, P * t0:P * t1].bitcast(FP8X4), scales=w1_scales[b, a][:, P * t0:P * t1],
+                                  in_=parts[1][:, t0:t1, :].rearrange("p t c -> p (t c)"))
 
         w2_codes, w3_codes = [], []
 
@@ -174,53 +176,50 @@ def tile_list_sign_variant_check_kernel(tc, tab_words, tab_scales, offs, w1, w2_
             w2_codes.append(codes2)
             w3_codes.append(codes3)
 
-        gather_words(0)
-        gather_bytes(0)
-        gather_bytes(1)
-        prepare_w1(0, 0, "vvvv", 4)
-        deal_w_scales(0, nc.vector.tensor_copy, I32)
-        prepare_w23(0)
-        gather_words(1)
-        prepare_w1(0, 1, "vvss", 1)
+        def row_constants():
+            vec_bank = bank()
+            for b in range(2):
+                nc.tensor.transpose(vec_bank[:, P * b:P * (b + 1)], row_vecs[:, P * b:P * (b + 1)], ident[:])
+            nc.scalar.copy(out=row_consts[:], in_=vec_bank[:, 0:2 * P].rearrange("p (b c) -> p b c", b=2)[:, :, 0:8])
 
-        vec_bank = bank()
-        for b in range(2):
-            nc.tensor.transpose(vec_bank[:, P * b:P * (b + 1)], row_vecs[:, P * b:P * (b + 1)], ident[:])
         row_consts = keep.tile([P, 2, 8], F32, name="row_consts")
-        nc.scalar.copy(out=row_consts[:], in_=vec_bank[:, 0:2 * P].rearrange("p (b c) -> p b c", b=2)[:, :, 0:8])
+        banks = {}
 
-        def product(lhs_codes, lhs_scales):
-            acc = bank()
-            for a in range(2):
-                nc.tensor.matmul_mx(out=acc[:], lhsT=lhs_codes(a), lhsT_scale=lhs_scales(a), rhs=picked[a][:].bitcast(FP8X4),
-                                    rhs_scale=picked_bytes[:, a, :], start=(a == 0), stop=(a == 1))
-            return acc
+        def product_pass(i, w, a):
+            b, t = divmod(i, 4)
+            col = 1024 * a + 512 * b + P * t
+            if w == 1:
+                codes, scales = w1_codes[b, a][:, P * t:P * (t + 1)].bitcast(FP8X4), w1_scales[b, a][:, P * t:P * (t + 1)]
+            elif w == 2:
+                codes, scales = w2_codes[b][:, a, 256 * t:256 * (t + 1)].bitcast(FP4X4), planes[:, col:col + P]
+            else:
+                codes, scales = w3_codes[b][:, a, P * t:P * (t + 1)].bitcast(FP8X4), planes[4:P, col:col + P]
+            if a == 0:
+                banks[i, w] = bank()
+            nc.tensor.matmul_mx(out=banks[i, w][:], lhsT=codes, lhsT_scale=scales, rhs=picked[a][:].bitcast(FP8X4),
+                                rhs_scale=picked_bytes[:, a, :], start=(a == 0), stop=(a == 1))
 
         sums = {}
         larger = {}
         feats = {}
 
+        def copy_second(i):
+            sums[i] = work.tile([P, S], F32, name="second_sb")
+            nc.scalar.copy(out=sums[i][:], in_=banks[i, 2][:])
+
         def first_products(i):
-            b, t = divmod(i, 4)
-            col = 512 * b + P * t
-            second = product(lambda a: w2_codes[b][:, a, 256 * t:256 * (t + 1)].bitcast(FP4X4),
-                             lambda a: planes[:, W2_PLANE + 1024 * a + col:W2_PLANE + 1024 * a + col + P])
-            third = product(lambda a: w3_codes[b][:, a, P * t:P * (t + 1)].bitcast(FP8X4),
-                            lambda a: planes[:, W3_PLANE + 1024 * a + col:W3_PLANE + 1024 * a + col + P])
-            first = product(lambda a: w1_codes[b, a][:, P * t:P * (t + 1)].bitcast(FP8X4),
-                            lambda a: w1_scales[b, a][:, P * t:P * (t + 1)])
-            second_sb = work.tile([P, S], F32, name="second_sb")
-            nc.scalar.copy(out=second_sb[:], in_=second[:])
-            sums[i] = (first, second_sb, third)
+            for w in (2, 1, 3):
+                for a in range(2):
+                    product_pass(i, w, a)
+            copy_second(i)
 
         def take_max(i):
-            first, second_sb, third = sums[i]
             larger[i] = work.tile([P, S], F32, name="larger")
-            nc.vector.tensor_tensor(out=larger[i][:], in0=first[:], in1=second_sb[:], op=ALU.max)
+            nc.vector.tensor_tensor(out=larger[i][:], in0=banks[i, 1][:], in1=sums[i][:], op=ALU.max)
 
         def take_off(i):
             feats[i] = work.tile([P, S], F32, name="feat", bufs=3)
-            nc.vector.tensor_tensor(out=feats[i][:], in0=larger[i][:], in1=sums[i][2][:], op=ALU.subtract)
+            nc.vector.tensor_tensor(out=feats[i][:], in0=larger[i][:], in1=banks[i, 3][:], op=ALU.subtract)
 
         def scatter(i):
             nc.vector.tensor_tensor(out=pages[i][:].indirect(list2[:]), in0=feats[i][:], in1=wgs_rows[:, i % 4, :], op=ALU.mult)
@@ -238,28 +237,30 @@ def tile_list_sign_variant_check_kernel(tc, tab_words, tab_scales, offs, w1, w2_
             b, t = divmod(i, 4)
             nc.scalar.copy(out=page_pairs[b][:, t // 2, :, t % 2], in_=pages[i][:])
 
-        def fetch(i):
-            heads[i] = work.tile([P, NP], F32, name="head")
-            nc.vector.tensor_copy(out=heads[i][:], in_=pages[i][:].indirect(list3[:]))
+        def fetch(i, cols):
+            if cols.start == 0:
+                heads[i] = work.tile([P, NP], F32, name="head")
+            nc.vector.tensor_copy(out=heads[i][:, cols], in_=pages[i][:].indirect(list3[:, cols.start // 16:cols.stop // 16]))
 
-        def bend(i):
+        def bend(i, cols):
             b, t = divmod(i, 4)
-            bent[i] = work.tile([P, NP], F32, name="bent")
-            nc.vector.scalar_tensor_tensor(out=bent[i][:], in0=heads[i][:], scalar=row_consts[:, b, t:t + 1], in1=heads[i][:],
-                                           op0=ALU.mult, op1=ALU.max)
+            if cols.start == 0:
+                bent[i] = work.tile([P, NP], F32, name="bent")
+            nc.vector.scalar_tensor_tensor(out=bent[i][:, cols], in0=heads[i][:, cols], scalar=row_consts[:, b, t:t + 1],
+                                           in1=heads[i][:, cols], op0=ALU.mult, op1=ALU.max)
 
-        def round_x(i):
+        def round_x(i, cols):
             b, t = divmod(i, 4)
-            dst = x_pairs[b][:, t // 2, :, t % 2]
+            dst = x_pairs[b][:, t // 2, cols, t % 2]
             factor = row_consts[:, b, 4 + t:5 + t]
             if i >= 6:
-                nc.vector.tensor_scalar(out=dst, in0=bent[i][:], scalar1=factor, scalar2=None, op0=ALU.mult)
+                nc.vector.tensor_scalar(out=dst, in0=bent[i][:, cols], scalar1=factor, scalar2=None, op0=ALU.mult)
             else:
-                nc.scalar.activation(out=dst, in_=bent[i][:], func=ACT.Copy, scale=factor)
+                nc.scalar.activation(out=dst, in_=bent[i][:, cols], func=ACT.Copy, scale=factor)
 
         def weave(pairs, cols, engine_copy, word=U32):
             width = cols.stop - cols.start
-            woven = work.tile([P, 4 * width], BF16, name="woven", bufs=4, align_bytes=64)
+            woven = work.tile([P, 4 * width], BF16, name="woven%d" % width, bufs=3 if width == 512 else 6, align_bytes=64)
             words = pairs[:].rearrange("p u c e -> p u (c e)").bitcast(word)[:, :, cols]
             engine_copy(out=woven[:].bitcast(word).rearrange("p (c u) -> p c u", u=2), in_=words.rearrange("p u c -> p c u"))
             return woven
@@ -267,30 +268,63 @@ def tile_list_sign_variant_check_kernel(tc, tab_words, tab_scales, offs, w1, w2_
         def quantise(woven, codes, scales, cols):
             nc.vector.quantize_mx(out=codes[:, cols].bitcast(FP8X4), scales=scales[:, cols], in_=woven[:])
 
-        first_products(0)
+        gather_words(0)
+        gather_bytes(0)
+        gather_bytes(1)
+        parts = w1_tiles(0, 0)
+        for t in range(4):
+            round_w1(parts, t, nc.vector.tensor_copy)
+        deal_w_scales(0, nc.vector.tensor_copy, I32)
+        quantise_w1(0, 0, parts, 0, 4)
+        prepare_w23(0)
+        for i in range(2):
+            for w in (1, 2, 3):
+                product_pass(i, w, 0)
+        gather_words(1)
+        for i in range(2):
+            for w in (2, 3):
+                product_pass(i, w, 1)
+            copy_second(i)
+        parts = w1_tiles(0, 1)
+        for t in range(4):
+            round_w1(parts, t, nc.vector.tensor_copy if t < 2 else nc.scalar.copy)
+        for i in range(2):
+            quantise_w1(0, 1, parts, i, i + 1)
+            product_pass(i, 1, 1)
         take_max(0)
-        take_off(0)
-        first_products(1)
         take_max(1)
-        take_off(1)
+        take_off(0)
+        quantise_w1(0, 1, parts, 2, 4)
+        row_constants()
         woven_pages, woven_x = {}, {}
+        whole, halves = slice(0, NP), (slice(0, NP // 2), slice(NP // 2, NP))
         for i in range(8):
-            if i == 1:
-                prepare_w23(1)
-                deal_w_scales(1, nc.scalar.copy, U32)
-                prepare_w1(1, 0, "ssss", 4)
-            if i == 2:
-                prepare_w1(1, 1, "ssss", 4)
-            scatter(i)
-            round_page(i)
             if i + 2 < 8:
                 first_products(i + 2)
-                take_max(i + 2)
-            fetch(i)
+            if i < 2:
+                parts = w1_tiles(1, i)
+                for t in range(4):
+                    round_w1(parts, t, nc.scalar.copy)
+            if i == 1:
+                deal_w_scales(1, nc.scalar.copy, U32)
+                prepare_w23(1)
+            scatter(i)
+            if i == 0:
+                take_off(1)
+            round_page(i)
             if i + 2 < 8:
+                take_max(i + 2)
+            if i + 2 < 8:
+                fetch(i, whole)
                 take_off(i + 2)
-            bend(i)
-            round_x(i)
+                bend(i, whole)
+                round_x(i, whole)
+            else:
+                for step in (fetch, bend, round_x):
+                    for cols in halves:
+                        step(i, cols)
+            if i < 2:
+                quantise_w1(1, i, parts, 0, 4)
             if i == 3:
                 for c in range(2):
                     woven_pages[c] = weave(page_pairs[0], slice(512 * c, 512 * (c + 1)), nc.scalar.copy)
@@ -308,17 +342,18 @@ def tile_list_sign_variant_check_kernel(tc, tab_words, tab_scales, offs, w1, w2_
         scores = [bank() for k in range(8)]
         for k in range(8):
             score(scores[k], 0, k)
-        woven_x[1] = weave(x_pairs[1], slice(0, NP), nc.vector.tensor_copy, I32)
+        last_x = [weave(x_pairs[1], cols, nc.vector.tensor_copy, I32) for cols in halves]
         for c in range(4):
             woven_pages[c] = weave(page_pairs[1], slice(256 * c, 256 * (c + 1)), nc.scalar.copy)
-        quantise(woven_pages[0], page_codes[1], page_scales[1], slice(0, 256))
-        quantise(woven_x[1], x_codes[1], x_scales[1], slice(0, NP))
-        for c in range(1, 4):
+        for cols, woven in zip(halves, last_x):
+            quantise(woven, x_codes[1], x_scales[1], cols)
+        for c in range(4):
             quantise(woven_pages[c], page_codes[1], page_scales[1], slice(256 * c, 256 * (c + 1)))
         for k in range(8):
             score(scores[k], 1, k)
             diff = work.tile([P, NP], F32, name="diff", bufs=3)
-            nc.vector.tensor_tensor(out=diff[:], in0=scores[k][:], in1=base_sb[k // 4][:, k % 4, :], op=ALU.subtract)
             result = work.tile([P, NP], F32, name="result", bufs=4)
-            nc.scalar.activation(out=result[:], in_=diff[:], func=ACT.Square)
-            nc.sync.dma_start(out=out[P * k:P * (k + 1), :], in_=result[:])
+            for cols in (halves if k == 7 else (whole,)):
+                nc.vector.tensor_tensor(out=diff[:, cols], in0=scores[k][:, cols], in1=base_sb[k // 4][:, k % 4, cols], op=ALU.subtract)
+                nc.scalar.activation(out=result[:, cols], in_=diff[:, cols], func=ACT.Square)
+                nc.sync.dma_start(out=out[P * k:P * (k + 1), cols], in_=result[:, cols])

from contextlib import ExitStack

import concourse.mybir as mybir
from concourse.masks import make_identity

K, H, T, S, T2, NP = 1024, 1024, 2048, 512, 1024, 512
FLOPS = 2 * 3 * K * H * S + 2 * H * T2 * NP

F32 = mybir.dt.float32
BF16 = mybir.dt.bfloat16
I32 = mybir.dt.int32
U32 = mybir.dt.uint32
U16 = mybir.dt.uint16
U8 = mybir.dt.uint8
FP8X4 = mybir.dt.float8_e4m3fn_x4
FP4X4 = mybir.dt.float4_e2m1fn_x4
ALU = mybir.AluOpType
ACT = mybir.ActivationFunctionType

P = 128
PLANES = 2048


def tile_list_sign_variant_check_kernel(tc, tab_words, tab_scales, offs, w1, w2_words, w2_scales,
                                                  w3_words, w3_scales, wgs, page0, offs2, offs3, gain, sense,
                                                  base, out):
    nc = tc.nc
    with ExitStack() as ctx:
        keep = ctx.enter_context(tc.tile_pool(name="keep", bufs=1))
        work = ctx.enter_context(tc.tile_pool(name="work", bufs=2))
        psum = ctx.enter_context(tc.psum_pool(name="psum", bufs=8))

        def bank():
            return psum.tile([P, 512], F32, name="bank")

        list1 = keep.tile([P, S // 16], U16, name="list1")
        list2 = keep.tile([P, S // 16], U16, name="list2")
        list3 = keep.tile([P, NP // 16], U16, name="list3")
        tab_bytes = keep.tile([P, 2, T], U8, name="tab_bytes", align_bytes=64)
        w_bytes = keep.tile([P, PLANES], U8, name="w_bytes", align_bytes=64)
        planes = keep.tile([P, PLANES], U8, name="planes", align_bytes=64)
        wgs_raw = keep.tile([P, S], F32, name="wgs_raw")
        row_vecs = keep.tile([P, 256], F32, name="row_vecs")
        ident = keep.tile([P, P], F32, name="ident")
        tab = [keep.tile([P, T], U32, name="tab%d" % a, align_bytes=64) for a in range(2)]
        pages = [keep.tile([P, T2], F32, name="page%d" % i) for i in range(8)]
        page_rows = page0.rearrange("(b g t j) m -> b t g j m", b=2, g=16, t=4, j=8)

        def load_w1(b, a):
            raw = work.tile([P, 4, 512], F32, name="big", bufs=3)
            nc.sync.dma_start(out=raw[:], in_=w1[512 * a:512 * (a + 1), 512 * b:512 * (b + 1)].rearrange("(p i) c -> p i c", i=4))
            return raw

        def load_w23(b):
            raw3 = work.tile([P, 2, 512], U32, name="w3_raw")
            nc.sync.dma_start(out=raw3[:].bitcast(I32),
                              in_=w3_words[:, :, 512 * b:512 * (b + 1), :].rearrange("a p c i -> p a (c i)").bitcast(I32))
            raw2 = work.tile([P, 2, 256], U32, name="w2_raw")
            nc.sync.dma_start(out=raw2[:].bitcast(I32),
                              in_=w2_words[:, :, 1024 * b:1024 * (b + 1)].rearrange("a p c -> p a c").bitcast(I32))
            return raw2, raw3

        def load_tab(a):
            nc.sync.dma_start(out=tab[a][:].bitcast(I32), in_=tab_words[a].rearrange("p t i -> p (t i)").bitcast(I32))

        def load_page(i):
            nc.sync.dma_start(out=pages[i][:], in_=page_rows[i // 4, i % 4])

        def load_w_scales(quadrants):
            for w, scales in enumerate((w2_scales, w3_scales)):
                for q in quadrants:
                    nc.sync.dma_start(out=w_bytes[32 * q + 4 * w:32 * q + 4 * w + 4, :].rearrange("r (a c) -> r a c", a=2).bitcast(I32),
                                      in_=scales[:, 4 * q:4 * q + 4, :].rearrange("a r c -> r a c").bitcast(I32))

        nc.gpsimd.memset(row_vecs[:], 0.0)
        load_tab(0)
        nc.sync.dma_start(out=wgs_raw[:], in_=wgs)
        nc.sync.dma_start(out=list1[:], in_=offs)
        w1_raw = {(0, 0): load_w1(0, 0)}
        load_w_scales((0, 2))
        w23_raw = [load_w23(0)]
        load_w_scales((1, 3))
        load_tab(1)
        w1_raw[0, 1] = load_w1(0, 1)
        load_page(0)
        nc.sync.dma_start(out=list2[:], in_=offs2)
        nc.sync.dma_start(out=list3[:], in_=offs3)
        nc.vector.memset(tab_bytes[:].bitcast(I32), 0)
        nc.vector.memset(planes[:].bitcast(I32), 0)
        for v, vec in enumerate((gain, sense)):
            nc.sync.dma_start(out=row_vecs[4 * v:4 * v + 4, :].rearrange("t (x j) -> t x j", j=8),
                              in_=vec.rearrange("(x t j) -> t x j", t=4, j=8))
        base_sb = []

        def load_base(half):
            rows = work.tile([P, 4, 512], F32, name="big", bufs=3)
            nc.sync.dma_start(out=rows[:], in_=base[512 * half:512 * (half + 1), :].rearrange("(k p) n -> p k n", p=P))
            base_sb.append(rows)

        w1_raw[1, 0] = load_w1(1, 0)
        load_page(1)
        w1_raw[1, 1] = load_w1(1, 1)
        w23_raw.append(load_w23(1))
        load_base(0)
        for i in range(2, 8):
            load_page(i)
        load_base(1)

        make_identity(nc, ident[:])
        for q in (0, 2, 1, 3):
            nc.gpsimd.dma_start(out=tab_bytes[32 * q:32 * q + 4].bitcast(I32),
                                in_=tab_scales[:, 4 * q:4 * q + 4, :].rearrange("a r t -> r a t").bitcast(I32))
        picked_bytes = keep.tile([P, 2, S], U8, name="picked_bytes", align_bytes=64)

        def gather_bytes(a):
            nc.vector.tensor_copy(out=picked_bytes[:, a, :], in_=tab_bytes[:, a, :].indirect(list1[:]))

        def deal_w_scales(b, engine_copy, word):
            for q in range(4):
                rows = slice(32 * q, 32 * q + 8)
                dst = planes[rows].bitcast(word).rearrange("r (x b t g w) -> r b x t g w", b=2, t=4, g=16, w=2)
                src = w_bytes[rows].bitcast(word).rearrange("r (x b g t w) -> r b x t g w", b=2, t=4, g=16, w=2)
                engine_copy(out=dst[:, b], in_=src[:, b])

        turned = bank()
        for c in range(4):
            nc.tensor.transpose(turned[:, P * c:P * (c + 1)], wgs_raw[:, P * c:P * (c + 1)], ident[:])
        wgs_cols = keep.tile([P, 4, 4, P], F32, name="wgs_cols")
        for c in range(4):
            src = turned[:, P * c:P * (c + 1)].rearrange("j (g t i) -> j t g i", g=4, t=4).unsqueeze(2).to_broadcast([P, 4, 4, 4, 8])
            nc.scalar.copy(out=wgs_cols[:, c].rearrange("j t (q g i) -> j t q g i", q=4, g=4), in_=src)
        wgs_rows = keep.tile([P, 4, S], F32, name="wgs_rows")
        for t in range(4):
            back = bank()
            for c in range(4):
                nc.tensor.transpose(back[:, P * c:P * (c + 1)], wgs_cols[:, c, t, :], ident[:])
            nc.scalar.copy(out=wgs_rows[:, t, :], in_=back[:])

        picked = []
        for a in range(2):
            words = keep.tile([P, S], U32, name="picked%d" % a, align_bytes=64)
            picked.append(words)

        def gather_words(a):
            nc.vector.tensor_copy(out=picked[a][:], in_=tab[a][:].indirect(list1[:]))

        w1_codes = {}
        w1_scales = {}

        def w1_tiles(b, a):
            raw = w1_raw[b, a][:].rearrange("p i (g t j) -> p t g j i", g=16, t=4)
            grouped = work.tile([P, 4, 512], BF16, name="w1_bf16", align_bytes=64)
            codes = keep.tile([P, 512], U32, name="w1_codes%d%d" % (b, a), align_bytes=64)
            scales = keep.tile([P, 512], U8, name="w1_scales%d%d" % (b, a), align_bytes=64)
            w1_codes[b, a], w1_scales[b, a] = codes, scales
            return raw, grouped

        def round_w1(parts, t, engine_copy):
            raw, grouped = parts
            engine_copy(out=grouped[:, t, :].rearrange("p (g j i) -> p g j i", g=16, j=8), in_=raw[:, t])

        def quantise_w1(b, a, parts, t0, t1):
            nc.vector.quantize_mx(out=w1_codes[b, a][:, P * t0:P * t1].bitcast(FP8X4), scales=w1_scales[b, a][:, P * t0:P * t1],
                                  in_=parts[1][:, t0:t1, :].rearrange("p t c -> p (t c)"))

        w2_codes, w3_codes = [], []

        def prepare_w23(b):
            raw2, raw3 = w23_raw[b]
            codes2 = keep.tile([P, 2, 1024], U8, name="w2_codes%d" % b, align_bytes=64)
            nc.scalar.copy(out=codes2[:].bitcast(U32).rearrange("p a (t g w) -> p a t g w", t=4, g=16),
                           in_=raw2[:].rearrange("p a (g t w) -> p a t g w", t=4, g=16))
            codes3 = keep.tile([P, 2, 512], U32, name="w3_codes%d" % b, align_bytes=64)
            nc.scalar.copy(out=codes3[:].rearrange("p a (t g w) -> p a t g w", t=4, g=16),
                           in_=raw3[:].rearrange("p a (g t w) -> p a t g w", t=4, g=16))
            w2_codes.append(codes2)
            w3_codes.append(codes3)

        def row_constants():
            vec_bank = bank()
            for b in range(2):
                nc.tensor.transpose(vec_bank[:, P * b:P * (b + 1)], row_vecs[:, P * b:P * (b + 1)], ident[:])
            nc.scalar.copy(out=row_consts[:], in_=vec_bank[:, 0:2 * P].rearrange("p (b c) -> p b c", b=2)[:, :, 0:8])

        row_consts = keep.tile([P, 2, 8], F32, name="row_consts")
        banks = {}

        def product_pass(i, w, a):
            b, t = divmod(i, 4)
            col = 1024 * a + 512 * b + P * t
            if w == 1:
                codes, scales = w1_codes[b, a][:, P * t:P * (t + 1)].bitcast(FP8X4), w1_scales[b, a][:, P * t:P * (t + 1)]
            elif w == 2:
                codes, scales = w2_codes[b][:, a, 256 * t:256 * (t + 1)].bitcast(FP4X4), planes[:, col:col + P]
            else:
                codes, scales = w3_codes[b][:, a, P * t:P * (t + 1)].bitcast(FP8X4), planes[4:P, col:col + P]
            if a == 0:
                banks[i, w] = bank()
            nc.tensor.matmul_mx(out=banks[i, w][:], lhsT=codes, lhsT_scale=scales, rhs=picked[a][:].bitcast(FP8X4),
                                rhs_scale=picked_bytes[:, a, :], start=(a == 0), stop=(a == 1))

        sums = {}
        larger = {}
        feats = {}

        def copy_second(i):
            sums[i] = work.tile([P, S], F32, name="second_sb")
            nc.scalar.copy(out=sums[i][:], in_=banks[i, 2][:])

        def first_products(i):
            for w in (2, 1, 3):
                for a in range(2):
                    product_pass(i, w, a)
            copy_second(i)

        def take_max(i):
            larger[i] = work.tile([P, S], F32, name="larger")
            nc.vector.tensor_tensor(out=larger[i][:], in0=banks[i, 1][:], in1=sums[i][:], op=ALU.max)

        def take_off(i):
            feats[i] = work.tile([P, S], F32, name="feat", bufs=3)
            nc.vector.tensor_tensor(out=feats[i][:], in0=larger[i][:], in1=banks[i, 3][:], op=ALU.subtract)

        def scatter(i):
            nc.vector.tensor_tensor(out=pages[i][:].indirect(list2[:]), in0=feats[i][:], in1=wgs_rows[:, i % 4, :], op=ALU.mult)

        page_pairs = [work.tile([P, 2, T2, 2], BF16, name="page_pairs", bufs=1, align_bytes=64) for b in range(2)]
        x_pairs = [work.tile([P, 2, NP, 2], BF16, name="x_pairs", bufs=1, align_bytes=64) for b in range(2)]
        page_codes = [keep.tile([P, T2], U32, name="page_codes%d" % b, align_bytes=64) for b in range(2)]
        page_scales = [keep.tile([P, T2], U8, name="page_scales%d" % b, align_bytes=64) for b in range(2)]
        x_codes = [keep.tile([P, NP], U32, name="x_codes%d" % b, align_bytes=64) for b in range(2)]
        x_scales = [keep.tile([P, NP], U8, name="x_scales%d" % b, align_bytes=64) for b in range(2)]
        heads = {}
        bent = {}

        def round_page(i):
            b, t = divmod(i, 4)
            nc.scalar.copy(out=page_pairs[b][:, t // 2, :, t % 2], in_=pages[i][:])

        def fetch(i, cols):
            if cols.start == 0:
                heads[i] = work.tile([P, NP], F32, name="head")
            nc.vector.tensor_copy(out=heads[i][:, cols], in_=pages[i][:].indirect(list3[:, cols.start // 16:cols.stop // 16]))

        def bend(i, cols):
            b, t = divmod(i, 4)
            if cols.start == 0:
                bent[i] = work.tile([P, NP], F32, name="bent")
            nc.vector.scalar_tensor_tensor(out=bent[i][:, cols], in0=heads[i][:, cols], scalar=row_consts[:, b, t:t + 1],
                                           in1=heads[i][:, cols], op0=ALU.mult, op1=ALU.max)

        def round_x(i, cols):
            b, t = divmod(i, 4)
            dst = x_pairs[b][:, t // 2, cols, t % 2]
            factor = row_consts[:, b, 4 + t:5 + t]
            if i >= 6:
                nc.vector.tensor_scalar(out=dst, in0=bent[i][:, cols], scalar1=factor, scalar2=None, op0=ALU.mult)
            else:
                nc.scalar.activation(out=dst, in_=bent[i][:, cols], func=ACT.Copy, scale=factor)

        def weave(pairs, cols, engine_copy, word=U32):
            width = cols.stop - cols.start
            woven = work.tile([P, 4 * width], BF16, name="woven%d" % width, bufs=3 if width == 512 else 6, align_bytes=64)
            words = pairs[:].rearrange("p u c e -> p u (c e)").bitcast(word)[:, :, cols]
            engine_copy(out=woven[:].bitcast(word).rearrange("p (c u) -> p c u", u=2), in_=words.rearrange("p u c -> p c u"))
            return woven

        def quantise(woven, codes, scales, cols):
            nc.vector.quantize_mx(out=codes[:, cols].bitcast(FP8X4), scales=scales[:, cols], in_=woven[:])

        gather_words(0)
        gather_bytes(0)
        gather_bytes(1)
        parts = w1_tiles(0, 0)
        for t in range(4):
            round_w1(parts, t, nc.vector.tensor_copy)
        deal_w_scales(0, nc.vector.tensor_copy, I32)
        quantise_w1(0, 0, parts, 0, 4)
        prepare_w23(0)
        for i in range(2):
            for w in (1, 2, 3):
                product_pass(i, w, 0)
        gather_words(1)
        for i in range(2):
            for w in (2, 3):
                product_pass(i, w, 1)
            copy_second(i)
        parts = w1_tiles(0, 1)
        for t in range(4):
            round_w1(parts, t, nc.vector.tensor_copy if t < 2 else nc.scalar.copy)
        for i in range(2):
            quantise_w1(0, 1, parts, i, i + 1)
            product_pass(i, 1, 1)
        take_max(0)
        take_max(1)
        take_off(0)
        quantise_w1(0, 1, parts, 2, 4)
        row_constants()
        woven_pages, woven_x = {}, {}
        whole, halves = slice(0, NP), (slice(0, NP // 2), slice(NP // 2, NP))
        for i in range(8):
            if i + 2 < 8:
                first_products(i + 2)
            if i < 2:
                parts = w1_tiles(1, i)
                for t in range(4):
                    round_w1(parts, t, nc.scalar.copy)
            if i == 1:
                deal_w_scales(1, nc.scalar.copy, U32)
                prepare_w23(1)
            scatter(i)
            if i == 0:
                take_off(1)
            round_page(i)
            if i + 2 < 8:
                take_max(i + 2)
            if i + 2 < 8:
                fetch(i, whole)
                take_off(i + 2)
                bend(i, whole)
                round_x(i, whole)
            else:
                for step in (fetch, bend, round_x):
                    for cols in halves:
                        step(i, cols)
            if i < 2:
                quantise_w1(1, i, parts, 0, 4)
            if i == 3:
                for c in range(2):
                    woven_pages[c] = weave(page_pairs[0], slice(512 * c, 512 * (c + 1)), nc.scalar.copy)
                woven_x[0] = weave(x_pairs[0], slice(0, NP), nc.scalar.copy)
            if i == 4:
                for c in range(2):
                    quantise(woven_pages[c], page_codes[0], page_scales[0], slice(512 * c, 512 * (c + 1)))
                quantise(woven_x[0], x_codes[0], x_scales[0], slice(0, NP))

        def score(acc, b, k):
            nc.tensor.matmul_mx(out=acc[:], lhsT=page_codes[b][:, P * k:P * (k + 1)].bitcast(FP8X4),
                                lhsT_scale=page_scales[b][:, P * k:P * (k + 1)], rhs=x_codes[b][:].bitcast(FP8X4),
                                rhs_scale=x_scales[b][:], start=(b == 0), stop=(b == 1))

        scores = [bank() for k in range(8)]
        for k in range(8):
            score(scores[k], 0, k)
        last_x = [weave(x_pairs[1], cols, nc.vector.tensor_copy, I32) for cols in halves]
        for c in range(4):
            woven_pages[c] = weave(page_pairs[1], slice(256 * c, 256 * (c + 1)), nc.scalar.copy)
        for cols, woven in zip(halves, last_x):
            quantise(woven, x_codes[1], x_scales[1], cols)
        for c in range(4):
            quantise(woven_pages[c], page_codes[1], page_scales[1], slice(256 * c, 256 * (c + 1)))
        for k in range(8):
            score(scores[k], 1, k)
            diff = work.tile([P, NP], F32, name="diff", bufs=3)
            result = work.tile([P, NP], F32, name="result", bufs=4)
            for cols in (halves if k == 7 else (whole,)):
                nc.vector.tensor_tensor(out=diff[:, cols], in0=scores[k][:, cols], in1=base_sb[k // 4][:, k % 4, cols], op=ALU.subtract)
                nc.scalar.activation(out=result[:, cols], in_=diff[:, cols], func=ACT.Square)
                nc.sync.dma_start(out=out[P * k:P * (k + 1), cols], in_=result[:, cols])
